import numpy as np
import ml_dtypes


def mxq(x, axis, fmt="e4m3"):
    dtype, down = {"e4m3": (ml_dtypes.float8_e4m3fn, 7), "e5m2": (ml_dtypes.float8_e5m2, 14)}[fmt]
    v = np.moveaxis(np.asarray(x, np.float32).astype(ml_dtypes.bfloat16).astype(np.float64), axis, -1)
    blocks = v.reshape(v.shape[:-1] + (-1, 32))
    amax = np.abs(blocks).max(-1, keepdims=True)
    byte = np.maximum(np.where(amax > 0, np.frexp(amax)[1] - 1 + 127, 0) - down, 1)
    scale = np.exp2(byte - 127.0)
    codes = (blocks / scale).astype(np.float32).astype(dtype).astype(np.float64)
    return np.moveaxis((codes * scale).reshape(v.shape), -1, axis)


WIDE = False


def mx_kscale(k):
    if not WIDE:
        return np.ones(k)
    levels = np.array([10, -10, 5, -5, 0])
    if k % 512:
        return np.exp2(np.random.permutation(np.resize(levels, k // 32))).repeat(32)
    a = np.empty((k // 512, 16))
    for p in range(k // 512):
        a[p, :8] = np.random.permutation(np.resize(levels, 8))
        for g in range(8):
            far = levels[np.abs(levels - a[p, g]) >= 10]
            a[p, g + 8] = far[np.random.randint(len(far))]
    return np.exp2(a.ravel()).repeat(32)


def f64(x):
    return np.asarray(x).astype(np.float64)


def striped(idx):
    return np.tile(np.asarray(idx).reshape(-1, 16).T, (8, 1)).astype(np.uint16)


def unstriped(offs):
    return offs[:16].T.reshape(-1).astype(np.int64)


E2M1 = np.array([0.0, 0.5, 1.0, 1.5, 2.0, 3.0, 4.0, 6.0, -0.0, -0.5, -1.0, -1.5, -2.0, -3.0, -4.0, -6.0])


def pack_weight(w, fmt):
    k, n = w.shape
    w = f64(np.asarray(w, np.float32).astype(ml_dtypes.bfloat16)).reshape(k // 32, 32, n)
    amax = np.abs(w).max(1)
    if fmt == "e4m3":
        byte = np.frexp(amax)[1] - 1 + 127 - 7
    else:
        mant, ex = np.frexp(amax / 6.0)
        byte = np.where(mant > 0.5, ex, ex - 1) + 127
    byte = np.clip(np.where(amax > 0, byte, 1), 1, 254)
    scaled = (w * np.exp2(127.0 - byte)[:, None, :]).reshape(k, n).astype(np.float32)
    by_word = np.ascontiguousarray(scaled.reshape(k // 512, 128, 4, n).transpose(0, 1, 3, 2))
    if fmt == "e4m3":
        words = by_word.astype(ml_dtypes.float8_e4m3fn).view(np.uint8)
    else:
        c = by_word.astype(ml_dtypes.float4_e2m1fn).view(np.uint8) & 0xF
        words = (c[..., 0::2] | (c[..., 1::2] << 4)).reshape(k // 512, 128, 2 * n)
    return np.ascontiguousarray(words), np.ascontiguousarray(byte.astype(np.uint8).reshape(k // 512, 16, n))


def unpack_weight(words, scales, fmt):
    g, _, n = scales.shape
    words = np.ascontiguousarray(words).reshape(g, 128, n, -1)
    if fmt == "e4m3":
        vals = words.view(ml_dtypes.float8_e4m3fn).astype(np.float64)
    else:
        nib = np.empty((g, 128, n, 4), np.uint8)
        nib[..., 0::2] = words & 0xF
        nib[..., 1::2] = words >> 4
        vals = E2M1[nib]
    vals = vals * np.repeat(np.exp2(scales.astype(np.float64) - 127.0), 8, axis=1)[..., None]
    return vals.transpose(0, 1, 3, 2).reshape(g * 512, n)


def bf(x):
    return np.asarray(x, np.float32).astype(ml_dtypes.bfloat16)


def planes(Y):
    r, m = Y.shape
    b = f64(bf(Y)).reshape(r // 32, 32, m)
    amax = np.abs(b).max(1)
    byte = np.clip(np.where(amax > 0, np.frexp(amax)[1] - 1 + 127 - 7, 1), 1, 254)
    codes = (b * np.exp2(127.0 - byte)[:, None, :]).reshape(r, m).astype(np.float32).astype(ml_dtypes.float8_e4m3fn).view(np.uint8)
    words = codes.reshape(r // 512, 128, 4, m).transpose(0, 1, 3, 2)
    return np.ascontiguousarray(words), np.ascontiguousarray(byte.astype(np.uint8).reshape(r // 512, 16, m))


K, T, J, I, R, N = 512, 2048, 1024, 512, 512, 512


def setup_inputs():
    n = np.random.standard_normal
    idx = np.random.permutation(T)[:J]
    fk = mx_kscale(K)
    fr = mx_kscale(R)
    xtp = pack_weight(n((K, T)) / fk[:, None], "e2m1")
    wap = pack_weight(n((K, R)) * 1 / np.sqrt(K) * fk[:, None] * fr, "e4m3")
    wbp = pack_weight(n((R, N)) * 1 / np.sqrt(R) / fr[:, None], "e2m1")
    wcp = pack_weight(n((R, N)) * 1 / np.sqrt(R) / fr[:, None], "e4m3")
    return {
        "xt_words": xtp[0],
        "xt_scales": xtp[1],
        "wa_words": wap[0],
        "wa_scales": wap[1],
        "wb_words": wbp[0],
        "wb_scales": wbp[1],
        "wc_words": wcp[0],
        "wc_scales": wcp[1],
        "offs": striped(idx),
    }


def reference(xt_words, xt_scales, wa_words, wa_scales, wb_words, wb_scales, wc_words, wc_scales, offs):
    idx = unstriped(offs)
    xtu = unpack_weight(xt_words, xt_scales, "e2m1")
    wau = unpack_weight(wa_words, wa_scales, "e4m3")
    wbu = unpack_weight(wb_words, wb_scales, "e2m1")
    wcu = unpack_weight(wc_words, wc_scales, "e4m3")
    xtidxg = xtu[:, idx]
    a = wau.T @ xtidxg
    h1 = np.maximum(a, 0.0)
    ha = h1[:, 0:0 + I]
    hb = h1[:, 512:512 + I]
    haq = mxq(ha, 0, "e4m3")
    hbq = mxq(hb, 0, "e4m3")
    p = wbu.T @ haq + wcu.T @ hbq
    y = np.tanh(0.7 * p)
    words, scales = planes(y)
    return y, words, scales

@@ -1,0 +1,182 @@
+from contextlib import ExitStack
+
+import concourse.mybir as mybir
+
+K, T, J, I, R, N = 512, 2048, 1024, 512, 512, 512
+FLOPS = 2 * K * R * J + 2 * 2 * R * N * I
+
+F32 = mybir.dt.float32
+BF16 = mybir.dt.bfloat16
+I32 = mybir.dt.int32
+U32 = mybir.dt.uint32
+U16 = mybir.dt.uint16
+U8 = mybir.dt.uint8
+FP8X4 = mybir.dt.float8_e4m3fn_x4
+FP4X4 = mybir.dt.float4_e2m1fn_x4
+ACT = mybir.ActivationFunctionType
+
+P = 128
+PACK = 4
+CHUNK = 128
+PIECE = 256
+
+
+def load_scale_rows(queue, tile, scales, first):
+    for q in range(4):
+        queue.dma_start(
+            out=tile[32 * q + first : 32 * q + first + 4, :].bitcast(I32),
+            in_=scales[0, 4 * q : 4 * q + 4, :].bitcast(I32),
+        )
+
+
+def deal(nc, dealt, raw):
+    nc.vector.tensor_copy(
+        out=dealt.rearrange("p (t m) -> p m t", t=PACK),
+        in_=raw.rearrange("p (m t) -> p m t", t=PACK),
+    )
+
+
+def tile_list_halves_as_partners_pl_kernel(
+    tc, xt_words, xt_scales, wa_words, wa_scales, wb_words, wb_scales, wc_words, wc_scales, offs, out_0, out_1, out_2
+):
+    nc = tc.nc
+    with ExitStack() as ctx:
+        keep = ctx.enter_context(tc.tile_pool(name="keep", bufs=1))
+        shared = ctx.enter_context(tc.tile_pool(name="shared", bufs=1))
+        psum1 = ctx.enter_context(tc.psum_pool(name="psum1", bufs=4))
+        psum2 = ctx.enter_context(tc.psum_pool(name="psum2", bufs=1))
+
+        offsets = keep.tile([P, J // 16], U16, name="offsets")
+        xw = keep.tile([P, T], U16, name="xw", align_bytes=64)
+        xs = keep.tile([P, T], U8, name="xs", align_bytes=64)
+        wa_raw = keep.tile([P, R], I32, name="wa_raw", align_bytes=64)
+        wb_raw = keep.tile([P, N], U16, name="wb_raw", align_bytes=64)
+        wc_raw = keep.tile([P, N], I32, name="wc_raw", align_bytes=64)
+        sa_raw = shared.tile([P, R], U8, name="sa_raw", align_bytes=64, offset=256)
+        sbc_raw = keep.tile([P, N], U8, name="sbc_raw", align_bytes=64)
+        wa = keep.tile([P, R], I32, name="wa", align_bytes=64)
+        wb = keep.tile([P, N], U16, name="wb", align_bytes=64)
+        wc = keep.tile([P, N], I32, name="wc", align_bytes=64)
+        sa = keep.tile([P, R], U8, name="sa", align_bytes=64)
+        sbc = keep.tile([P, N], U8, name="sbc", align_bytes=64)
+        warm = keep.tile([P, 2], F32, name="warm")
+
+        nc.vector.memset(xs[:].bitcast(I32), 0)
+        nc.vector.memset(sa_raw[:].bitcast(I32), 0)
+        nc.vector.memset(sbc_raw[:].bitcast(I32), 0)
+        nc.vector.memset(warm[:], 0.0)
+
+        nc.sync.dma_start(offsets[:], offs)
+        load_scale_rows(nc.scalar, xs, xt_scales, 0)
+        nc.sync.dma_start(out=xw[:].bitcast(I32), in_=xt_words[0].bitcast(I32))
+        nc.sync.dma_start(out=wa_raw[:], in_=wa_words[0].rearrange("p n t -> p (n t)").bitcast(I32))
+        load_scale_rows(nc.sync, sa_raw, wa_scales, 0)
+        nc.scalar.activation(out=warm[:, 1:2], in_=warm[:, 0:1], func=ACT.Tanh)
+        nc.sync.dma_start(out=wb_raw[:].bitcast(I32), in_=wb_words[0].bitcast(I32))
+        nc.sync.dma_start(out=wc_raw[:], in_=wc_words[0].rearrange("p n t -> p (n t)").bitcast(I32))
+        load_scale_rows(nc.sync, sbc_raw, wb_scales, 0)
+        load_scale_rows(nc.sync, sbc_raw, wc_scales, 4)
+
+        n_chunks = I // CHUNK
+        acc2 = [psum2.tile([P, PACK, CHUNK], F32, name="acc2_%d" % c) for c in range(n_chunks)]
+        y_codes = keep.tile([P, I], U32, name="y_codes", align_bytes=64)
+        y_scales = keep.tile([P, I], U8, name="y_scales", align_bytes=64)
+        y_rows = out_0.rearrange("(p t) i -> p t i", t=PACK)
+        codes_out = out_1[0].rearrange("p i t -> p (i t)").bitcast(I32)
+
+        def gather(out, window, j0):
+            nc.vector.tensor_copy(out, window[:].indirect(offsets[:, j0 // 16 : (j0 + PIECE) // 16]))
+
+        def layer1(gw, gs, j0, on_vector):
+            acc = psum1.tile([P, PACK, CHUNK], F32, name="acc1")
+            for t in range(PACK):
+                nc.tensor.matmul_mx(
+                    out=acc[:, t, :],
+                    lhsT=wa[:, t * P : (t + 1) * P].bitcast(FP8X4),
+                    lhsT_scale=sa[:, t * P : (t + 1) * P],
+                    rhs=gw.bitcast(FP4X4),
+                    rhs_scale=gs,
+                    start=True,
+                    stop=True,
+                )
+            h = keep.tile([P, CHUNK, PACK], BF16, name="h_%d" % j0, align_bytes=64)
+            if on_vector:
+                nc.vector.tensor_scalar_max(h[:], acc[:].rearrange("p t j -> p j t"), 0.0)
+            else:
+                nc.scalar.activation(out=h[:], in_=acc[:].rearrange("p t j -> p j t"), func=ACT.Relu)
+            return h
+
+        def quantize_h(h, j0):
+            hq = keep.tile([P, CHUNK], U32, name="hq_%d" % j0, align_bytes=64)
+            hs = keep.tile([P, CHUNK], U8, name="hs_%d" % j0, align_bytes=64)
+            nc.vector.quantize_mx(out=hq[:].bitcast(FP8X4), scales=hs[:], in_=h[:].rearrange("p j t -> p (j t)"))
+            return hq, hs
+
+        def layer2(c, hq, hs, partner):
+            for t in range(PACK):
+                cols = slice(t * P, (t + 1) * P)
+                nc.tensor.matmul_mx(
+                    out=acc2[c][:, t, :],
+                    lhsT=wc[:, cols].bitcast(FP8X4) if partner else wb[:, cols].bitcast(FP4X4),
+                    lhsT_scale=sbc[4:P, cols] if partner else sbc[:, cols],
+                    rhs=hq[:].bitcast(FP8X4),
+                    rhs_scale=hs[:],
+                    start=(not partner and t == 0),
+                    stop=(partner and t == PACK - 1),
+                )
+
+        def finish(c):
+            cols = slice(c * CHUNK, (c + 1) * CHUNK)
+            y = keep.tile([P, PACK, CHUNK], F32, name="y_%d" % c)
+            nc.scalar.activation(out=y[:], in_=acc2[c][:], func=ACT.Tanh, scale=0.7)
+            nc.sync.dma_start(out=y_rows[:, :, cols], in_=y[:])
+            yb = keep.tile([P, CHUNK, PACK], BF16, name="yb_%d" % c, align_bytes=64)
+            nc.vector.tensor_copy(out=yb[:], in_=y[:].rearrange("p t i -> p i t"))
+            return yb
+
+        def planes(c, yb):
+            cols = slice(c * CHUNK, (c + 1) * CHUNK)
+            nc.vector.quantize_mx(
+                out=y_codes[:, cols].bitcast(FP8X4), scales=y_scales[:, cols], in_=yb[:].rearrange("p i t -> p (i t)")
+            )
+            nc.sync.dma_start(out=codes_out[:, cols], in_=y_codes[:, cols].bitcast(I32))
+
+        gs_early = keep.tile([P, 2, PIECE], U8, name="gs_early", align_bytes=64)
+        gw_early = keep.tile([P, PIECE], U16, name="gw_early", align_bytes=64)
+        gather(gs_early[:, 0, :], xs, 0)
+        gather(gs_early[:, 1, :], xs, I)
+        gather(gw_early[:], xw, 0)
+        deal(nc, wa[:], wa_raw[:])
+        deal(nc, sa[:], sa_raw[:])
+        gs_late = shared.tile([P, 2, PIECE], U8, name="gs_late", align_bytes=64, offset=0)
+        gw_late = shared.tile([P, 3, PIECE], U16, name="gw_late", align_bytes=64, offset=512)
+        gather(gw_late[:, 0, :], xw, I)
+        gather(gs_late[:, 0, :], xs, PIECE)
+        gather(gw_late[:, 1, :], xw, PIECE)
+        gather(gs_late[:, 1, :], xs, I + PIECE)
+        gather(gw_late[:, 2, :], xw, I + PIECE)
+        pieces = [
+            (0, gw_early[:], gs_early[:, 0, :]),
+            (I, gw_late[:, 0, :], gs_early[:, 1, :]),
+            (PIECE, gw_late[:, 1, :], gs_late[:, 0, :]),
+            (I + PIECE, gw_late[:, 2, :], gs_late[:, 1, :]),
+        ]
+        hs_bf = {}
+        for j0, gw, gs in pieces:
+            for c0 in range(0, PIECE, CHUNK):
+                hs_bf[j0 + c0] = layer1(gw[:, c0 : c0 + CHUNK], gs[:, c0 : c0 + CHUNK], j0 + c0, False)
+        deal(nc, wb[:], wb_raw[:])
+        deal(nc, sbc[:], sbc_raw[:])
+        deal(nc, wc[:], wc_raw[:])
+        for c in range(n_chunks):
+            for partner in (False, True):
+                j0 = c * CHUNK + (I if partner else 0)
+                hq, hs = quantize_h(hs_bf[j0], j0)
+                layer2(c, hq, hs, partner)
+        for c in range(n_chunks):
+            yb = finish(c)
+            planes(c, yb)
+        for q in range(4):
+            nc.sync.dma_start(
+                out=out_2[0, 4 * q : 4 * q + 4, :].bitcast(I32), in_=y_scales[32 * q : 32 * q + 4, :].bitcast(I32)
+            )

@@ -21,12 +21,11 @@ CHUNK = 128
 PIECE = 256
 
 
-def load_scale_rows(queue, tile, scales, first):
-    for q in range(4):
-        queue.dma_start(
-            out=tile[32 * q + first : 32 * q + first + 4, :].bitcast(I32),
-            in_=scales[0, 4 * q : 4 * q + 4, :].bitcast(I32),
-        )
+def load_scale_rows(queue, tile, scales, q, first=0):
+    queue.dma_start(
+        out=tile[32 * q + first : 32 * q + first + 4, :].bitcast(I32),
+        in_=scales[0, 4 * q : 4 * q + 4, :].bitcast(I32),
+    )
 
 
 def deal(nc, dealt, raw):
@@ -43,52 +42,59 @@ def tile_list_halves_as_partners_pl_kernel(
     with ExitStack() as ctx:
         keep = ctx.enter_context(tc.tile_pool(name="keep", bufs=1))
         shared = ctx.enter_context(tc.tile_pool(name="shared", bufs=1))
-        psum1 = ctx.enter_context(tc.psum_pool(name="psum1", bufs=4))
-        psum2 = ctx.enter_context(tc.psum_pool(name="psum2", bufs=1))
+        second = ctx.enter_context(tc.tile_pool(name="second", bufs=1))
+        window = ctx.enter_context(tc.tile_pool(name="window", bufs=1))
+        psum = ctx.enter_context(tc.psum_pool(name="psum", bufs=8))
 
         offsets = keep.tile([P, J // 16], U16, name="offsets")
         xw = keep.tile([P, T], U16, name="xw", align_bytes=64)
-        xs = keep.tile([P, T], U8, name="xs", align_bytes=64)
-        wa_raw = keep.tile([P, R], I32, name="wa_raw", align_bytes=64)
-        wb_raw = keep.tile([P, N], U16, name="wb_raw", align_bytes=64)
-        wc_raw = keep.tile([P, N], I32, name="wc_raw", align_bytes=64)
-        sa_raw = shared.tile([P, R], U8, name="sa_raw", align_bytes=64, offset=256)
-        sbc_raw = keep.tile([P, N], U8, name="sbc_raw", align_bytes=64)
+        xs = window.tile([P, T], U8, name="xs", align_bytes=64, offset=1024)
+        wa_raw = second.tile([P, R], I32, name="wa_raw", align_bytes=64, offset=1024)
+        sa_raw = shared.tile([P, R], U8, name="sa_raw", align_bytes=64, offset=512)
         wa = keep.tile([P, R], I32, name="wa", align_bytes=64)
-        wb = keep.tile([P, N], U16, name="wb", align_bytes=64)
-        wc = keep.tile([P, N], I32, name="wc", align_bytes=64)
         sa = keep.tile([P, R], U8, name="sa", align_bytes=64)
-        sbc = keep.tile([P, N], U8, name="sbc", align_bytes=64)
-        warm = keep.tile([P, 2], F32, name="warm")
+        sbc_raw = second.tile([P, N], U8, name="sbc_raw", align_bytes=64, offset=0)
+        warm = keep.tile([P, 8], F32, name="warm")
+
+        def gather(out, window, j0):
+            nc.vector.tensor_copy(out, window[:].indirect(offsets[:, j0 // 16 : (j0 + out.shape[1]) // 16]))
 
         nc.vector.memset(xs[:].bitcast(I32), 0)
-        nc.vector.memset(sa_raw[:].bitcast(I32), 0)
-        nc.vector.memset(sbc_raw[:].bitcast(I32), 0)
+        nc.gpsimd.memset(sa_raw[:].bitcast(I32), 0)
         nc.vector.memset(warm[:], 0.0)
+        nc.vector.memset(sbc_raw[:].bitcast(I32), 0)
 
         nc.sync.dma_start(offsets[:], offs)
-        load_scale_rows(nc.scalar, xs, xt_scales, 0)
         nc.sync.dma_start(out=xw[:].bitcast(I32), in_=xt_words[0].bitcast(I32))
         nc.sync.dma_start(out=wa_raw[:], in_=wa_words[0].rearrange("p n t -> p (n t)").bitcast(I32))
-        load_scale_rows(nc.sync, sa_raw, wa_scales, 0)
+        for q in range(4):
+            load_scale_rows(nc.scalar, xs, xt_scales, q)
+        for q in range(4):
+            load_scale_rows(nc.scalar if q < 2 else nc.gpsimd, sa_raw, wa_scales, q)
         nc.scalar.activation(out=warm[:, 1:2], in_=warm[:, 0:1], func=ACT.Tanh)
+        gs_a = keep.tile([P, I], U8, name="gs_a", align_bytes=64)
+        gw_first = keep.tile([P, PIECE], U16, name="gw_first", align_bytes=64)
+        gather(gw_first[:], xw, 0)
+        deal(nc, wa[:], wa_raw[:])
+        gather(gs_a[:], xs, 0)
+        for q in range(4):
+            load_scale_rows(nc.scalar, sbc_raw, wb_scales, q)
+        for q in range(4):
+            load_scale_rows(nc.scalar if q < 3 else nc.gpsimd, sbc_raw, wc_scales, q, 4)
+        wb_raw = second.tile([P, N], U16, name="wb_raw", align_bytes=64, offset=512)
+        wc_raw = second.tile([P, N], I32, name="wc_raw", align_bytes=64, offset=1536)
         nc.sync.dma_start(out=wb_raw[:].bitcast(I32), in_=wb_words[0].bitcast(I32))
         nc.sync.dma_start(out=wc_raw[:], in_=wc_words[0].rearrange("p n t -> p (n t)").bitcast(I32))
-        load_scale_rows(nc.sync, sbc_raw, wb_scales, 0)
-        load_scale_rows(nc.sync, sbc_raw, wc_scales, 4)
 
         n_chunks = I // CHUNK
-        acc2 = [psum2.tile([P, PACK, CHUNK], F32, name="acc2_%d" % c) for c in range(n_chunks)]
+        acc2 = []
         y_codes = keep.tile([P, I], U32, name="y_codes", align_bytes=64)
         y_scales = keep.tile([P, I], U8, name="y_scales", align_bytes=64)
         y_rows = out_0.rearrange("(p t) i -> p t i", t=PACK)
         codes_out = out_1[0].rearrange("p i t -> p (i t)").bitcast(I32)
 
-        def gather(out, window, j0):
-            nc.vector.tensor_copy(out, window[:].indirect(offsets[:, j0 // 16 : (j0 + PIECE) // 16]))
-
-        def layer1(gw, gs, j0, on_vector):
-            acc = psum1.tile([P, PACK, CHUNK], F32, name="acc1")
+        def layer1(gw, gs, h):
+            acc = psum.tile([P, PACK, CHUNK], F32, name="acc")
             for t in range(PACK):
                 nc.tensor.matmul_mx(
                     out=acc[:, t, :],
@@ -99,83 +105,92 @@ def tile_list_halves_as_partners_pl_kernel(
                     start=True,
                     stop=True,
                 )
-            h = keep.tile([P, CHUNK, PACK], BF16, name="h_%d" % j0, align_bytes=64)
-            if on_vector:
-                nc.vector.tensor_scalar_max(h[:], acc[:].rearrange("p t j -> p j t"), 0.0)
-            else:
-                nc.scalar.activation(out=h[:], in_=acc[:].rearrange("p t j -> p j t"), func=ACT.Relu)
-            return h
+            nc.scalar.activation(out=h, in_=acc[:].rearrange("p t j -> p j t"), func=ACT.Relu)
 
-        def quantize_h(h, j0):
-            hq = keep.tile([P, CHUNK], U32, name="hq_%d" % j0, align_bytes=64)
-            hs = keep.tile([P, CHUNK], U8, name="hs_%d" % j0, align_bytes=64)
-            nc.vector.quantize_mx(out=hq[:].bitcast(FP8X4), scales=hs[:], in_=h[:].rearrange("p j t -> p (j t)"))
-            return hq, hs
+        def quantize_h(j0, width):
+            nc.vector.quantize_mx(
+                out=h_codes[j0 // I][:, j0 % I : j0 % I + width].bitcast(FP8X4),
+                scales=h_scales[:, j0 : j0 + width],
+                in_=h_bf[:, j0 : j0 + width, :].rearrange("p j t -> p (j t)"),
+            )
 
-        def layer2(c, hq, hs, partner):
+        def layer2(c, partner):
+            j0 = c * CHUNK + (I if partner else 0)
             for t in range(PACK):
                 cols = slice(t * P, (t + 1) * P)
                 nc.tensor.matmul_mx(
                     out=acc2[c][:, t, :],
                     lhsT=wc[:, cols].bitcast(FP8X4) if partner else wb[:, cols].bitcast(FP4X4),
                     lhsT_scale=sbc[4:P, cols] if partner else sbc[:, cols],
-                    rhs=hq[:].bitcast(FP8X4),
-                    rhs_scale=hs[:],
+                    rhs=h_codes[1 if partner else 0][:, c * CHUNK : (c + 1) * CHUNK].bitcast(FP8X4),
+                    rhs_scale=h_scales[:, j0 : j0 + CHUNK],
                     start=(not partner and t == 0),
                     stop=(partner and t == PACK - 1),
                 )
 
-        def finish(c):
-            cols = slice(c * CHUNK, (c + 1) * CHUNK)
-            y = keep.tile([P, PACK, CHUNK], F32, name="y_%d" % c)
-            nc.scalar.activation(out=y[:], in_=acc2[c][:], func=ACT.Tanh, scale=0.7)
-            nc.sync.dma_start(out=y_rows[:, :, cols], in_=y[:])
-            yb = keep.tile([P, CHUNK, PACK], BF16, name="yb_%d" % c, align_bytes=64)
-            nc.vector.tensor_copy(out=yb[:], in_=y[:].rearrange("p t i -> p i t"))
-            return yb
+        def result(c, y):
+            nc.scalar.activation(out=y, in_=acc2[c][:], func=ACT.Tanh, scale=0.7)
 
-        def planes(c, yb):
+        def planes(c, y):
             cols = slice(c * CHUNK, (c + 1) * CHUNK)
+            yb = keep.tile([P, CHUNK, PACK], BF16, name="yb_%d" % c, align_bytes=64)
+            if y is None:
+                nc.scalar.activation(out=yb[:], in_=acc2[c][:].rearrange("p t i -> p i t"), func=ACT.Tanh, scale=0.7)
+            else:
+                nc.vector.tensor_copy(
+                    out=yb[:].rearrange("p (c i) t -> p c t i", i=PACK),
+                    in_=y.rearrange("p t (c i) -> p c t i", i=PACK),
+                )
             nc.vector.quantize_mx(
                 out=y_codes[:, cols].bitcast(FP8X4), scales=y_scales[:, cols], in_=yb[:].rearrange("p i t -> p (i t)")
             )
-            nc.sync.dma_start(out=codes_out[:, cols], in_=y_codes[:, cols].bitcast(I32))
 
-        gs_early = keep.tile([P, 2, PIECE], U8, name="gs_early", align_bytes=64)
-        gw_early = keep.tile([P, PIECE], U16, name="gw_early", align_bytes=64)
-        gather(gs_early[:, 0, :], xs, 0)
-        gather(gs_early[:, 1, :], xs, I)
-        gather(gw_early[:], xw, 0)
-        deal(nc, wa[:], wa_raw[:])
         deal(nc, sa[:], sa_raw[:])
-        gs_late = shared.tile([P, 2, PIECE], U8, name="gs_late", align_bytes=64, offset=0)
-        gw_late = shared.tile([P, 3, PIECE], U16, name="gw_late", align_bytes=64, offset=512)
-        gather(gw_late[:, 0, :], xw, I)
-        gather(gs_late[:, 0, :], xs, PIECE)
-        gather(gw_late[:, 1, :], xw, PIECE)
-        gather(gs_late[:, 1, :], xs, I + PIECE)
-        gather(gw_late[:, 2, :], xw, I + PIECE)
-        pieces = [
-            (0, gw_early[:], gs_early[:, 0, :]),
-            (I, gw_late[:, 0, :], gs_early[:, 1, :]),
-            (PIECE, gw_late[:, 1, :], gs_late[:, 0, :]),
-            (I + PIECE, gw_late[:, 2, :], gs_late[:, 1, :]),
-        ]
-        hs_bf = {}
-        for j0, gw, gs in pieces:
-            for c0 in range(0, PIECE, CHUNK):
-                hs_bf[j0 + c0] = layer1(gw[:, c0 : c0 + CHUNK], gs[:, c0 : c0 + CHUNK], j0 + c0, False)
+        gs_b = shared.tile([P, I], U8, name="gs_b", align_bytes=64, offset=256)
+        gw_late = shared.tile([P, J - PIECE], U16, name="gw_late", align_bytes=64, offset=768)
+        gather(gw_late[:, 0:PIECE], xw, PIECE)
+        gather(gs_b[:], xs, I)
+        gather(gw_late[:, PIECE : 2 * PIECE], xw, I)
+        gather(gw_late[:, 2 * PIECE : 3 * PIECE], xw, I + PIECE)
+        h_bf = keep.tile([P, J, PACK], BF16, name="h_bf", align_bytes=64)
+        h_scales = keep.tile([P, J], U8, name="h_scales", align_bytes=64)
+        for j0 in range(0, J, CHUNK):
+            gw = gw_first[:, j0 : j0 + CHUNK] if j0 < PIECE else gw_late[:, j0 - PIECE : j0 - PIECE + CHUNK]
+            gs = gs_a[:, j0 : j0 + CHUNK] if j0 < I else gs_b[:, j0 - I : j0 - I + CHUNK]
+            layer1(gw, gs, h_bf[:, j0 : j0 + CHUNK, :])
+        wb = window.tile([P, N], U16, name="wb", align_bytes=64, offset=512)
+        sbc = window.tile([P, N], U8, name="sbc", align_bytes=64, offset=1536)
+        wc = window.tile([P, N], I32, name="wc", align_bytes=64, offset=2048)
         deal(nc, wb[:], wb_raw[:])
         deal(nc, sbc[:], sbc_raw[:])
         deal(nc, wc[:], wc_raw[:])
+        h_codes = [second.tile([P, I], U32, name="ha_codes", align_bytes=64, offset=0)]
         for c in range(n_chunks):
-            for partner in (False, True):
-                j0 = c * CHUNK + (I if partner else 0)
-                hq, hs = quantize_h(hs_bf[j0], j0)
-                layer2(c, hq, hs, partner)
-        for c in range(n_chunks):
-            yb = finish(c)
-            planes(c, yb)
+            acc2.append(psum.tile([P, PACK, CHUNK], F32, name="acc"))
+        quantize_h(0, PIECE)
+        layer2(0, False)
+        layer2(1, False)
+        h_codes.append(second.tile([P, I], U32, name="hb_codes", align_bytes=64, offset=2048))
+        quantize_h(I, PIECE)
+        layer2(0, True)
+        layer2(1, True)
+        quantize_h(PIECE, PIECE)
+        layer2(2, False)
+        layer2(3, False)
+        for c in (2, 3):
+            quantize_h(I + c * CHUNK, CHUNK)
+            layer2(c, True)
+        ys = [keep.tile([P, PACK, CHUNK], F32, name="y_%d" % c) for c in range(n_chunks)]
+        for c in range(n_chunks - 1):
+            result(c, ys[c][:])
+            nc.sync.dma_start(out=y_rows[:, :, c * CHUNK : (c + 1) * CHUNK], in_=ys[c][:])
+            planes(c, ys[c][:])
+        y3 = ys[3]
+        nc.sync.dma_start(out=codes_out[:, 0 : 3 * CHUNK], in_=y_codes[:, 0 : 3 * CHUNK].bitcast(I32))
+        planes(3, None)
+        result(3, y3[:])
+        nc.sync.dma_start(out=codes_out[:, 3 * CHUNK : I], in_=y_codes[:, 3 * CHUNK : I].bitcast(I32))
+        nc.scalar.dma_start(out=y_rows[:, :, 3 * CHUNK : I], in_=y3[:])
         for q in range(4):
             nc.sync.dma_start(
                 out=out_2[0, 4 * q : 4 * q + 4, :].bitcast(I32), in_=y_scales[32 * q : 32 * q + 4, :].bitcast(I32)

from contextlib import ExitStack

import concourse.mybir as mybir

K, T, J, I, R, N = 512, 2048, 1024, 512, 512, 512
FLOPS = 2 * K * R * J + 2 * 2 * R * N * I

F32 = mybir.dt.float32
BF16 = mybir.dt.bfloat16
I32 = mybir.dt.int32
U32 = mybir.dt.uint32
U16 = mybir.dt.uint16
U8 = mybir.dt.uint8
FP8X4 = mybir.dt.float8_e4m3fn_x4
FP4X4 = mybir.dt.float4_e2m1fn_x4
ACT = mybir.ActivationFunctionType

P = 128
PACK = 4
CHUNK = 128
PIECE = 256


def load_scale_rows(queue, tile, scales, q, first=0):
    queue.dma_start(
        out=tile[32 * q + first : 32 * q + first + 4, :].bitcast(I32),
        in_=scales[0, 4 * q : 4 * q + 4, :].bitcast(I32),
    )


def deal(nc, dealt, raw):
    nc.vector.tensor_copy(
        out=dealt.rearrange("p (t m) -> p m t", t=PACK),
        in_=raw.rearrange("p (m t) -> p m t", t=PACK),
    )


def tile_list_halves_as_partners_pl_kernel(
    tc, xt_words, xt_scales, wa_words, wa_scales, wb_words, wb_scales, wc_words, wc_scales, offs, out_0, out_1, out_2
):
    nc = tc.nc
    with ExitStack() as ctx:
        keep = ctx.enter_context(tc.tile_pool(name="keep", bufs=1))
        shared = ctx.enter_context(tc.tile_pool(name="shared", bufs=1))
        second = ctx.enter_context(tc.tile_pool(name="second", bufs=1))
        window = ctx.enter_context(tc.tile_pool(name="window", bufs=1))
        psum = ctx.enter_context(tc.psum_pool(name="psum", bufs=8))

        offsets = keep.tile([P, J // 16], U16, name="offsets")
        xw = keep.tile([P, T], U16, name="xw", align_bytes=64)
        xs = window.tile([P, T], U8, name="xs", align_bytes=64, offset=1024)
        wa_raw = second.tile([P, R], I32, name="wa_raw", align_bytes=64, offset=1024)
        sa_raw = shared.tile([P, R], U8, name="sa_raw", align_bytes=64, offset=512)
        wa = keep.tile([P, R], I32, name="wa", align_bytes=64)
        sa = keep.tile([P, R], U8, name="sa", align_bytes=64)
        sbc_raw = second.tile([P, N], U8, name="sbc_raw", align_bytes=64, offset=0)
        warm = keep.tile([P, 8], F32, name="warm")

        def gather(out, window, j0):
            nc.vector.tensor_copy(out, window[:].indirect(offsets[:, j0 // 16 : (j0 + out.shape[1]) // 16]))

        nc.vector.memset(xs[:].bitcast(I32), 0)
        nc.gpsimd.memset(sa_raw[:].bitcast(I32), 0)
        nc.vector.memset(warm[:], 0.0)
        nc.vector.memset(sbc_raw[:].bitcast(I32), 0)

        nc.sync.dma_start(offsets[:], offs)
        nc.sync.dma_start(out=xw[:].bitcast(I32), in_=xt_words[0].bitcast(I32))
        nc.sync.dma_start(out=wa_raw[:], in_=wa_words[0].rearrange("p n t -> p (n t)").bitcast(I32))
        for q in range(4):
            load_scale_rows(nc.scalar, xs, xt_scales, q)
        for q in range(4):
            load_scale_rows(nc.scalar if q < 2 else nc.gpsimd, sa_raw, wa_scales, q)
        nc.scalar.activation(out=warm[:, 1:2], in_=warm[:, 0:1], func=ACT.Tanh)
        gs_a = keep.tile([P, I], U8, name="gs_a", align_bytes=64)
        gw_first = keep.tile([P, PIECE], U16, name="gw_first", align_bytes=64)
        gather(gw_first[:], xw, 0)
        deal(nc, wa[:], wa_raw[:])
        gather(gs_a[:], xs, 0)
        for q in range(4):
            load_scale_rows(nc.scalar, sbc_raw, wb_scales, q)
        for q in range(4):
            load_scale_rows(nc.scalar if q < 3 else nc.gpsimd, sbc_raw, wc_scales, q, 4)
        wb_raw = second.tile([P, N], U16, name="wb_raw", align_bytes=64, offset=512)
        wc_raw = second.tile([P, N], I32, name="wc_raw", align_bytes=64, offset=1536)
        nc.sync.dma_start(out=wb_raw[:].bitcast(I32), in_=wb_words[0].bitcast(I32))
        nc.sync.dma_start(out=wc_raw[:], in_=wc_words[0].rearrange("p n t -> p (n t)").bitcast(I32))

        n_chunks = I // CHUNK
        acc2 = []
        y_codes = keep.tile([P, I], U32, name="y_codes", align_bytes=64)
        y_scales = keep.tile([P, I], U8, name="y_scales", align_bytes=64)
        y_rows = out_0.rearrange("(p t) i -> p t i", t=PACK)
        codes_out = out_1[0].rearrange("p i t -> p (i t)").bitcast(I32)

        def layer1(gw, gs, h):
            acc = psum.tile([P, PACK, CHUNK], F32, name="acc")
            for t in range(PACK):
                nc.tensor.matmul_mx(
                    out=acc[:, t, :],
                    lhsT=wa[:, t * P : (t + 1) * P].bitcast(FP8X4),
                    lhsT_scale=sa[:, t * P : (t + 1) * P],
                    rhs=gw.bitcast(FP4X4),
                    rhs_scale=gs,
                    start=True,
                    stop=True,
                )
            nc.scalar.activation(out=h, in_=acc[:].rearrange("p t j -> p j t"), func=ACT.Relu)

        def quantize_h(j0, width):
            nc.vector.quantize_mx(
                out=h_codes[j0 // I][:, j0 % I : j0 % I + width].bitcast(FP8X4),
                scales=h_scales[:, j0 : j0 + width],
                in_=h_bf[:, j0 : j0 + width, :].rearrange("p j t -> p (j t)"),
            )

        def layer2(c, partner):
            j0 = c * CHUNK + (I if partner else 0)
            for t in range(PACK):
                cols = slice(t * P, (t + 1) * P)
                nc.tensor.matmul_mx(
                    out=acc2[c][:, t, :],
                    lhsT=wc[:, cols].bitcast(FP8X4) if partner else wb[:, cols].bitcast(FP4X4),
                    lhsT_scale=sbc[4:P, cols] if partner else sbc[:, cols],
                    rhs=h_codes[1 if partner else 0][:, c * CHUNK : (c + 1) * CHUNK].bitcast(FP8X4),
                    rhs_scale=h_scales[:, j0 : j0 + CHUNK],
                    start=(not partner and t == 0),
                    stop=(partner and t == PACK - 1),
                )

        def result(c, y):
            nc.scalar.activation(out=y, in_=acc2[c][:], func=ACT.Tanh, scale=0.7)

        def planes(c, y):
            cols = slice(c * CHUNK, (c + 1) * CHUNK)
            yb = keep.tile([P, CHUNK, PACK], BF16, name="yb_%d" % c, align_bytes=64)
            if y is None:
                nc.scalar.activation(out=yb[:], in_=acc2[c][:].rearrange("p t i -> p i t"), func=ACT.Tanh, scale=0.7)
            else:
                nc.vector.tensor_copy(
                    out=yb[:].rearrange("p (c i) t -> p c t i", i=PACK),
                    in_=y.rearrange("p t (c i) -> p c t i", i=PACK),
                )
            nc.vector.quantize_mx(
                out=y_codes[:, cols].bitcast(FP8X4), scales=y_scales[:, cols], in_=yb[:].rearrange("p i t -> p (i t)")
            )

        deal(nc, sa[:], sa_raw[:])
        gs_b = shared.tile([P, I], U8, name="gs_b", align_bytes=64, offset=256)
        gw_late = shared.tile([P, J - PIECE], U16, name="gw_late", align_bytes=64, offset=768)
        gather(gw_late[:, 0:PIECE], xw, PIECE)
        gather(gs_b[:], xs, I)
        gather(gw_late[:, PIECE : 2 * PIECE], xw, I)
        gather(gw_late[:, 2 * PIECE : 3 * PIECE], xw, I + PIECE)
        h_bf = keep.tile([P, J, PACK], BF16, name="h_bf", align_bytes=64)
        h_scales = keep.tile([P, J], U8, name="h_scales", align_bytes=64)
        for j0 in range(0, J, CHUNK):
            gw = gw_first[:, j0 : j0 + CHUNK] if j0 < PIECE else gw_late[:, j0 - PIECE : j0 - PIECE + CHUNK]
            gs = gs_a[:, j0 : j0 + CHUNK] if j0 < I else gs_b[:, j0 - I : j0 - I + CHUNK]
            layer1(gw, gs, h_bf[:, j0 : j0 + CHUNK, :])
        wb = window.tile([P, N], U16, name="wb", align_bytes=64, offset=512)
        sbc = window.tile([P, N], U8, name="sbc", align_bytes=64, offset=1536)
        wc = window.tile([P, N], I32, name="wc", align_bytes=64, offset=2048)
        deal(nc, wb[:], wb_raw[:])
        deal(nc, sbc[:], sbc_raw[:])
        deal(nc, wc[:], wc_raw[:])
        h_codes = [second.tile([P, I], U32, name="ha_codes", align_bytes=64, offset=0)]
        for c in range(n_chunks):
            acc2.append(psum.tile([P, PACK, CHUNK], F32, name="acc"))
        quantize_h(0, PIECE)
        layer2(0, False)
        layer2(1, False)
        h_codes.append(second.tile([P, I], U32, name="hb_codes", align_bytes=64, offset=2048))
        quantize_h(I, PIECE)
        layer2(0, True)
        layer2(1, True)
        quantize_h(PIECE, PIECE)
        layer2(2, False)
        layer2(3, False)
        for c in (2, 3):
            quantize_h(I + c * CHUNK, CHUNK)
            layer2(c, True)
        ys = [keep.tile([P, PACK, CHUNK], F32, name="y_%d" % c) for c in range(n_chunks)]
        for c in range(n_chunks - 1):
            result(c, ys[c][:])
            nc.sync.dma_start(out=y_rows[:, :, c * CHUNK : (c + 1) * CHUNK], in_=ys[c][:])
            planes(c, ys[c][:])
        y3 = ys[3]
        nc.sync.dma_start(out=codes_out[:, 0 : 3 * CHUNK], in_=y_codes[:, 0 : 3 * CHUNK].bitcast(I32))
        planes(3, None)
        result(3, y3[:])
        nc.sync.dma_start(out=codes_out[:, 3 * CHUNK : I], in_=y_codes[:, 3 * CHUNK : I].bitcast(I32))
        nc.scalar.dma_start(out=y_rows[:, :, 3 * CHUNK : I], in_=y3[:])
        for q in range(4):
            nc.sync.dma_start(
                out=out_2[0, 4 * q : 4 * q + 4, :].bitcast(I32), in_=y_scales[32 * q : 32 * q + 4, :].bitcast(I32)
            )
